import numpy as np
import ml_dtypes


def mxq(x, axis, fmt="e4m3"):
    dtype, down = {"e4m3": (ml_dtypes.float8_e4m3fn, 7), "e5m2": (ml_dtypes.float8_e5m2, 14)}[fmt]
    v = np.moveaxis(np.asarray(x, np.float32).astype(ml_dtypes.bfloat16).astype(np.float64), axis, -1)
    blocks = v.reshape(v.shape[:-1] + (-1, 32))
    amax = np.abs(blocks).max(-1, keepdims=True)
    byte = np.maximum(np.where(amax > 0, np.frexp(amax)[1] - 1 + 127, 0) - down, 1)
    scale = np.exp2(byte - 127.0)
    codes = (blocks / scale).astype(np.float32).astype(dtype).astype(np.float64)
    return np.moveaxis((codes * scale).reshape(v.shape), -1, axis)


WIDE = False


def mx_kscale(k):
    if not WIDE:
        return np.ones(k)
    levels = np.array([10, -10, 5, -5, 0])
    if k % 512:
        return np.exp2(np.random.permutation(np.resize(levels, k // 32))).repeat(32)
    a = np.empty((k // 512, 16))
    for p in range(k // 512):
        a[p, :8] = np.random.permutation(np.resize(levels, 8))
        for g in range(8):
            far = levels[np.abs(levels - a[p, g]) >= 10]
            a[p, g + 8] = far[np.random.randint(len(far))]
    return np.exp2(a.ravel()).repeat(32)


def f64(x):
    return np.asarray(x).astype(np.float64)


def striped(idx):
    return np.tile(np.asarray(idx).reshape(-1, 16).T, (8, 1)).astype(np.uint16)


def unstriped(offs):
    return offs[:16].T.reshape(-1).astype(np.int64)


def striped8(idx):
    return np.asarray(idx).reshape(8, -1, 16).transpose(0, 2, 1).reshape(128, -1).astype(np.uint16)


def unstriped8(offs):
    return offs.reshape(8, 16, -1).transpose(0, 2, 1).reshape(8, -1).astype(np.int64)


def pick8(x, idx, run):
    r = np.arange(len(x))
    return x[r[:, None], idx[r % (8 * run) // run]]


E2M1 = np.array([0.0, 0.5, 1.0, 1.5, 2.0, 3.0, 4.0, 6.0, -0.0, -0.5, -1.0, -1.5, -2.0, -3.0, -4.0, -6.0])


def pack_weight(w, fmt):
    k, n = w.shape
    w = f64(np.asarray(w, np.float32).astype(ml_dtypes.bfloat16)).reshape(k // 32, 32, n)
    amax = np.abs(w).max(1)
    if fmt == "e4m3":
        byte = np.frexp(amax)[1] - 1 + 127 - 7
    else:
        mant, ex = np.frexp(amax / 6.0)
        byte = np.where(mant > 0.5, ex, ex - 1) + 127
    byte = np.clip(np.where(amax > 0, byte, 1), 1, 254)
    scaled = (w * np.exp2(127.0 - byte)[:, None, :]).reshape(k, n).astype(np.float32)
    by_word = np.ascontiguousarray(scaled.reshape(k // 512, 128, 4, n).transpose(0, 1, 3, 2))
    if fmt == "e4m3":
        words = by_word.astype(ml_dtypes.float8_e4m3fn).view(np.uint8)
    else:
        c = by_word.astype(ml_dtypes.float4_e2m1fn).view(np.uint8) & 0xF
        words = (c[..., 0::2] | (c[..., 1::2] << 4)).reshape(k // 512, 128, 2 * n)
    return np.ascontiguousarray(words), np.ascontiguousarray(byte.astype(np.uint8).reshape(k // 512, 16, n))


def unpack_weight(words, scales, fmt):
    g, _, n = scales.shape
    words = np.ascontiguousarray(words).reshape(g, 128, n, -1)
    if fmt == "e4m3":
        vals = words.view(ml_dtypes.float8_e4m3fn).astype(np.float64)
    else:
        nib = np.empty((g, 128, n, 4), np.uint8)
        nib[..., 0::2] = words & 0xF
        nib[..., 1::2] = words >> 4
        vals = E2M1[nib]
    vals = vals * np.repeat(np.exp2(scales.astype(np.float64) - 127.0), 8, axis=1)[..., None]
    return vals.transpose(0, 1, 3, 2).reshape(g * 512, n)


K, J, R, T, U, F, Z, M, O, C, N = 512, 256, 512, 512, 512, 2048, 512, 1024, 128, 512, 256


def setup_inputs():
    n = np.random.standard_normal
    idx = np.random.permutation(T)[:J]
    idx2 = np.stack([np.random.permutation(U)[:J] for _ in range(8)])
    idx3 = np.stack([np.random.permutation(F)[:R] for _ in range(8)])
    idx4 = np.random.permutation(M)[:J]
    idx5 = np.stack([np.random.permutation(C)[:J] for _ in range(8)])
    idx6 = np.stack([np.random.permutation(C)[:O] for _ in range(8)])
    idx7 = np.stack([np.random.permutation(C)[:O] for _ in range(8)])
    fk = mx_kscale(K)
    fz = mx_kscale(Z)
    fr = mx_kscale(R)
    xop = pack_weight(n((Z, M)) / fz[:, None], "e4m3")
    w2p = pack_weight(n((Z, R)) * 1 / np.sqrt(Z) * fz[:, None], "e2m1")
    wbp = pack_weight(n((R, N)) * 1 / np.sqrt(R) / fr[:, None], "e2m1")
    return {
        "ta": (np.random.randint(-7, 8, (K, T)).astype(np.float64)).astype(np.float32),
        "tb": (np.random.randint(-7, 8, (K, U)).astype(np.float64)).astype(np.float32),
        "ga": ((np.random.randint(10, 25, (K, 1)) / 64.0) * fk[:, None]).astype(np.float32),
        "gb": ((np.random.randint(4, 13, (K, 1)) / 64.0) * fk[:, None]).astype(np.float32),
        "ua": (np.random.randint(-7, 8, (K, F)).astype(np.float64)).astype(np.float32),
        "ha": ((np.random.randint(8, 25, (K, 1)) / 1024.0) / fk[:, None]).astype(np.float32),
        "xo_words": xop[0],
        "xo_scales": xop[1],
        "w2_words": w2p[0],
        "w2_scales": w2p[1],
        "sa": (np.random.uniform(0.5, 1.6, (R, 1)) * fr[:, None]).astype(np.float32),
        "sb": (np.random.uniform(0.5, 1.6, (R, 1)) * fr[:, None]).astype(np.float32),
        "wb_words": wbp[0],
        "wb_scales": wbp[1],
        "offs": striped(idx),
        "offs2": striped8(idx2),
        "offs3": striped8(idx3),
        "offs4": striped(idx4),
        "offs5": striped8(idx5),
        "offs6": striped8(idx6),
        "offs7": striped8(idx7),
    }


def reference(ta, tb, ga, gb, ua, ha, xo_words, xo_scales, w2_words, w2_scales, sa, sb, wb_words, wb_scales, offs, offs2, offs3, offs4, offs5, offs6, offs7):
    idx = unstriped(offs)
    idx2 = unstriped8(offs2)
    idx3 = unstriped8(offs3)
    idx4 = unstriped(offs4)
    idx5 = unstriped8(offs5)
    idx6 = unstriped8(offs6)
    idx7 = unstriped8(offs7)
    xou = unpack_weight(xo_words, xo_scales, "e4m3")
    w2u = unpack_weight(w2_words, w2_scales, "e2m1")
    wbu = unpack_weight(wb_words, wb_scales, "e2m1")
    xc = f64(ta)[:, idx] * f64(ga) + pick8(f64(tb), idx2, 64) * f64(gb)
    wc = pick8(f64(ua), idx3, 64) * f64(ha)
    wcq = mxq(wc, 0, "e4m3")
    xcq = mxq(xc, 0, "e4m3")
    xoidx4g = xou[:, idx4]
    a = wcq.T @ xcq + w2u.T @ xoidx4g
    pw = np.zeros((R, C))
    pw[np.arange(R)[:, None], idx5[np.arange(R) % 512 // 64]] = a
    hid = np.abs(pick8(pw, idx6, 64) * f64(sa) - pick8(pw, idx7, 64) * f64(sb))
    hidq = mxq(hid, 0, "e4m3")
    y = wbu.T @ hidq
    return y

@@ -1,0 +1,223 @@
+from contextlib import ExitStack
+
+import concourse.mybir as mybir
+
+K, J, R, T, U, F, Z, M, O, C, N = 512, 256, 512, 512, 512, 2048, 512, 1024, 128, 512, 256
+FLOPS = 2 * (K * R * J + Z * R * J + R * N * O)
+
+F32 = mybir.dt.float32
+BF16 = mybir.dt.bfloat16
+I32 = mybir.dt.int32
+U32 = mybir.dt.uint32
+U16 = mybir.dt.uint16
+U8 = mybir.dt.uint8
+FP8X4 = mybir.dt.float8_e4m3fn_x4
+FP4X4 = mybir.dt.float4_e2m1fn_x4
+ACT = mybir.ActivationFunctionType
+ALU = mybir.AluOpType
+
+P = 128
+PACK = 4
+HALF = J // 2
+
+
+def tile_picked_basedetail_codes_bank_boardpair_one_plain_kernel(
+    tc, ta, tb, ga, gb, ua, ha, xo_words, xo_scales, w2_words, w2_scales, sa, sb, wb_words, wb_scales,
+    offs, offs2, offs3, offs4, offs5, offs6, offs7, out,
+):
+    nc = tc.nc
+    with ExitStack() as ctx:
+        keep = ctx.enter_context(tc.tile_pool(name="keep", bufs=1))
+        psum = ctx.enter_context(tc.psum_pool(name="psum", bufs=1))
+
+        def sbuf(name, shape, dtype):
+            return keep.tile(shape, dtype, name=name, align_bytes=64)
+
+        def load_list(name, src):
+            tile = sbuf(name, list(src.shape), U16)
+            nc.sync.dma_start(tile[:], src)
+            return tile
+
+        def load_column(name, src):
+            tile = sbuf(name, [P, PACK], F32)
+            nc.sync.dma_start(tile[:], src.rearrange("(p t) o -> p (t o)", t=PACK))
+            return tile
+
+        def load_rows(name, src, t):
+            tile = sbuf(name, [P, src.shape[1]], F32)
+            nc.sync.dma_start(tile[:], src.rearrange("(p t) c -> p t c", t=PACK)[:, t, :])
+            return tile
+
+        def load_scales(name, src, queue):
+            tile = sbuf(name, [P, src.shape[2]], U8)
+            nc.vector.memset(tile[:].bitcast(I32), 0)
+            for q in range(4):
+                queue.dma_start(tile[32 * q : 32 * q + 4, :].bitcast(I32), src[0, 4 * q : 4 * q + 4, :].bitcast(I32))
+            return tile
+
+        def stage_scales(name, src):
+            width = src.shape[2]
+            stage = sbuf(name + "_stage", [P, 2, width // 4], I32)
+            for u in range(2):
+                rows = src[0, 8 * u : 8 * u + 8, :].bitcast(I32).rearrange("(q r) c -> r q c", q=2)
+                nc.gpsimd.dma_start(stage[64 * u : 64 * u + 4, :, :], rows)
+            tile = sbuf(name, [P, width], U8)
+            nc.vector.memset(tile[:].bitcast(I32), 0)
+            for q in range(4):
+                u = q // 2
+                nc.vector.tensor_copy(out=tile[32 * q : 32 * q + 4, :].bitcast(I32), in_=stage[64 * u : 64 * u + 4, q % 2, :])
+            return tile
+
+        w2_sc = stage_scales("w2_sc", w2_scales)
+        xo_sc = stage_scales("xo_sc", xo_scales)
+
+        ua_sb = [load_rows("ua0", ua, 0)]
+        l3 = load_list("l3", offs3)
+        ha_sb = load_column("ha_sb", ha)
+        ua_sb.append(load_rows("ua1", ua, 1))
+        l1 = load_list("l1", offs)
+        ga_sb = load_column("ga_sb", ga)
+        l2 = load_list("l2", offs2)
+        gb_sb = load_column("gb_sb", gb)
+        ua_sb.append(load_rows("ua2", ua, 2))
+        ua_sb.append(load_rows("ua3", ua, 3))
+        l4 = load_list("l4", offs4)
+        ta_sb, tb_sb = [], []
+        for t in range(PACK):
+            ta_sb.append(load_rows("ta%d" % t, ta, t))
+            tb_sb.append(load_rows("tb%d" % t, tb, t))
+        w2_sb = sbuf("w2_sb", [P, 2 * R], U8)
+        nc.sync.dma_start(w2_sb[:].bitcast(I32), w2_words[0].bitcast(I32))
+        xo_sb = sbuf("xo_sb", [P, M], U32)
+        nc.sync.dma_start(xo_sb[:].bitcast(I32), xo_words[0].rearrange("p n t -> p (n t)").bitcast(I32))
+        l5 = load_list("l5", offs5)
+        l6 = load_list("l6", offs6)
+        sa_sb = load_column("sa_sb", sa)
+        l7 = load_list("l7", offs7)
+        sb_sb = load_column("sb_sb", sb)
+        wb_sb = sbuf("wb_sb", [P, 2 * N], U8)
+        nc.sync.dma_start(wb_sb[:].bitcast(I32), wb_words[0].bitcast(I32))
+        wb_sc = load_scales("wb_sc", wb_scales, nc.sync)
+
+        board = []
+        for s in range(PACK):
+            board.append(sbuf("board%d" % s, [P, C], F32))
+            nc.vector.memset(board[s][:], 0.0)
+
+        wc_planes = sbuf("wc_planes", [P, PACK, R], BF16)
+        for t in range(PACK):
+            nc.scalar.activation(out=wc_planes[:, t, :], in_=ua_sb[t][:].indirect(l3[:]), func=ACT.Copy, scale=ha_sb[:, t : t + 1])
+        w2_scd = sbuf("w2_scd", [P, R], U8)
+        nc.vector.tensor_copy(
+            out=w2_scd[:].rearrange("p (s m) -> p s m", s=PACK), in_=w2_sc[:].rearrange("p (m s) -> p s m", s=PACK)
+        )
+        xo_gsc = sbuf("xo_gsc", [P, J], U8)
+        nc.vector.tensor_copy(out=xo_gsc[:], in_=xo_sc[:].indirect(l4[:]))
+        wc_in = sbuf("wc_in", [P, R * PACK], BF16)
+        nc.vector.tensor_copy(
+            out=wc_in[:].rearrange("p (s m t) -> p m t s", s=PACK, t=PACK),
+            in_=wc_planes[:].rearrange("p t (m s) -> p m t s", s=PACK),
+        )
+        wc_q = sbuf("wc_q", [P, R], U32)
+        wc_sc = sbuf("wc_sc", [P, R], U8)
+        nc.vector.quantize_mx(out=wc_q[:].bitcast(FP8X4), scales=wc_sc[:], in_=wc_in[:])
+
+        xc_in = [sbuf("xc_in%d" % h, [P, HALF, PACK], BF16) for h in range(2)]
+        base01 = sbuf("base01", [P, 2, J], F32)
+        det01 = sbuf("det01", [P, 2, J], F32)
+        for t in range(2):
+            nc.scalar.activation(out=base01[:, t, :], in_=ta_sb[t][:].indirect(l1[:]), func=ACT.Copy, scale=ga_sb[:, t : t + 1])
+            nc.scalar.activation(out=det01[:, t, :], in_=tb_sb[t][:].indirect(l2[:]), func=ACT.Copy, scale=gb_sb[:, t : t + 1])
+        for h in range(2):
+            cols = slice(h * HALF, (h + 1) * HALF)
+            nc.vector.tensor_tensor(
+                out=xc_in[h][:, :, 0:2],
+                in0=base01[:, :, cols].rearrange("p t j -> p j t"),
+                in1=det01[:, :, cols].rearrange("p t j -> p j t"),
+                op=ALU.add,
+            )
+        base2 = sbuf("base2", [P, J], F32)
+        det2 = sbuf("det2", [P, J], F32)
+        base3 = sbuf("base3", [P, J], F32)
+        nc.scalar.activation(out=base2[:], in_=ta_sb[2][:].indirect(l1[:]), func=ACT.Copy, scale=ga_sb[:, 2:3])
+        nc.scalar.activation(out=det2[:], in_=tb_sb[2][:].indirect(l2[:]), func=ACT.Copy, scale=gb_sb[:, 2:3])
+        for h in range(2):
+            cols = slice(h * HALF, (h + 1) * HALF)
+            nc.vector.tensor_tensor(out=xc_in[h][:, :, 2], in0=base2[:, cols], in1=det2[:, cols], op=ALU.add)
+        nc.scalar.activation(out=base3[:], in_=ta_sb[3][:].indirect(l1[:]), func=ACT.Copy, scale=ga_sb[:, 3:4])
+        det3 = [sbuf("det3_%d" % h, [P, HALF], F32) for h in range(2)]
+        for h in range(2):
+            nc.scalar.activation(
+                out=det3[h][:], in_=tb_sb[3][:].indirect(l2[:, 8 * h : 8 * h + 8]), func=ACT.Copy, scale=gb_sb[:, 3:4]
+            )
+        for h in range(2):
+            cols = slice(h * HALF, (h + 1) * HALF)
+            nc.vector.tensor_tensor(out=xc_in[h][:, :, 3], in0=base3[:, cols], in1=det3[h][:], op=ALU.add)
+
+        w2_d = sbuf("w2_d", [P, 2 * R], U8)
+        nc.scalar.copy(
+            out=w2_d[:].bitcast(U16).rearrange("p (s m) -> p s m", s=PACK),
+            in_=w2_sb[:].bitcast(U16).rearrange("p (m s) -> p s m", s=PACK),
+        )
+
+        xc_q = sbuf("xc_q", [P, J], U32)
+        xc_sc = sbuf("xc_sc", [P, J], U8)
+        xo_g = sbuf("xo_g", [P, J], U32)
+        for h in range(2):
+            cols = slice(h * HALF, (h + 1) * HALF)
+            nc.vector.quantize_mx(
+                out=xc_q[:, cols].bitcast(FP8X4), scales=xc_sc[:, cols], in_=xc_in[h][:].rearrange("p j t -> p (j t)")
+            )
+            nc.vector.tensor_copy(out=xo_g[:, cols], in_=xo_sb[:].indirect(l4[:, 8 * h : 8 * h + 8]))
+
+        first = sbuf("first", [P, PACK - 1, O], F32)
+        second = sbuf("second", [P, PACK - 1, O], F32)
+        first_last = sbuf("first_last", [P, O], F32)
+        second_last = sbuf("second_last", [P, O], F32)
+        firsts = [first[:, s, :] for s in range(PACK - 1)] + [first_last[:]]
+        seconds = [second[:, s, :] for s in range(PACK - 1)] + [second_last[:]]
+        pieces = [(0, 0, HALF), (0, HALF, J)] + [(s, 0, J) for s in range(1, PACK)]
+        hidden = []
+        for i, (s, j0, j1) in enumerate(pieces):
+            rows = slice(s * P, (s + 1) * P)
+            acc = psum.tile([P, j1 - j0], F32, name="acc%d" % i, tag="acc", bufs=2)
+            nc.tensor.matmul_mx(
+                out=acc[:], lhsT=wc_q[:, rows].bitcast(FP8X4), lhsT_scale=wc_sc[:, rows],
+                rhs=xc_q[:, j0:j1].bitcast(FP8X4), rhs_scale=xc_sc[:, j0:j1], start=True, stop=False,
+            )
+            nc.tensor.matmul_mx(
+                out=acc[:], lhsT=w2_d[:, 2 * s * P : 2 * (s + 1) * P].bitcast(FP4X4), lhsT_scale=w2_scd[:, rows],
+                rhs=xo_g[:, j0:j1].bitcast(FP8X4), rhs_scale=xo_gsc[:, j0:j1], start=False, stop=True,
+            )
+            hidden.append(keep.tile([P, j1 - j0], F32, name="hidden%d" % i, tag="hidden", bufs=2, align_bytes=64))
+            nc.scalar.copy(out=hidden[i][:], in_=acc[:])
+            nc.vector.tensor_copy(out=board[s][:].indirect(l5[:, j0 // 16 : j1 // 16]), in_=hidden[i][:])
+        for s in range(PACK):
+            nc.scalar.activation(out=firsts[s], in_=board[s][:].indirect(l6[:]), func=ACT.Copy, scale=sa_sb[:, s : s + 1])
+            nc.scalar.activation(out=seconds[s], in_=board[s][:].indirect(l7[:]), func=ACT.Copy, scale=sb_sb[:, s : s + 1])
+
+        diff = sbuf("diff", [P, PACK, O], F32)
+        nc.vector.tensor_tensor(out=diff[:, 0:3, :], in0=first[:], in1=second[:], op=ALU.subtract)
+        nc.vector.tensor_tensor(out=diff[:, 3, :], in0=first_last[:], in1=second_last[:], op=ALU.subtract)
+        hid_in = sbuf("hid_in", [P, O, PACK], BF16)
+        for u in range(2):
+            nc.scalar.activation(
+                out=hid_in[:, :, 2 * u : 2 * u + 2], in_=diff[:, 2 * u : 2 * u + 2, :].rearrange("p s o -> p o s"), func=ACT.Abs
+            )
+        hid_q = sbuf("hid_q", [P, O], U32)
+        hid_sc = sbuf("hid_sc", [P, O], U8)
+        nc.vector.quantize_mx(out=hid_q[:].bitcast(FP8X4), scales=hid_sc[:], in_=hid_in[:].rearrange("p o s -> p (o s)"))
+
+        for h in range(2):
+            res = psum.tile([P, O], F32, name="res%d" % h)
+            nc.tensor.matmul_mx(
+                out=res[:], lhsT=wb_sb[:, 2 * h * P : 2 * (h + 1) * P].bitcast(FP4X4), lhsT_scale=wb_sc[:, h * P : (h + 1) * P],
+                rhs=hid_q[:].bitcast(FP8X4), rhs_scale=hid_sc[:], start=True, stop=True,
+            )
+            res_sb = sbuf("res_sb%d" % h, [P, O], F32)
+            if h == 0:
+                nc.vector.tensor_copy(out=res_sb[:], in_=res[:])
+                nc.sync.dma_start(out[h * P : (h + 1) * P, :], res_sb[:])
+            else:
+                nc.scalar.copy(out=res_sb[:], in_=res[:])
+                nc.scalar.dma_start(out[h * P : (h + 1) * P, :], res_sb[:])

@@ -77,20 +77,23 @@ def tile_picked_basedetail_codes_bank_boardpair_one_plain_kernel(
         ua_sb.append(load_rows("ua1", ua, 1))
         l1 = load_list("l1", offs)
         ga_sb = load_column("ga_sb", ga)
+        ta_sb = [load_rows("ta0", ta, 0)]
+        ua_sb.append(load_rows("ua2", ua, 2))
         l2 = load_list("l2", offs2)
         gb_sb = load_column("gb_sb", gb)
-        ua_sb.append(load_rows("ua2", ua, 2))
+        tb_sb = [load_rows("tb0", tb, 0)]
+        ta_sb.append(load_rows("ta1", ta, 1))
+        tb_sb.append(load_rows("tb1", tb, 1))
         ua_sb.append(load_rows("ua3", ua, 3))
         l4 = load_list("l4", offs4)
-        ta_sb, tb_sb = [], []
-        for t in range(PACK):
+        l5 = load_list("l5", offs5)
+        for t in range(2, PACK):
             ta_sb.append(load_rows("ta%d" % t, ta, t))
             tb_sb.append(load_rows("tb%d" % t, tb, t))
-        w2_sb = sbuf("w2_sb", [P, 2 * R], U8)
-        nc.sync.dma_start(w2_sb[:].bitcast(I32), w2_words[0].bitcast(I32))
         xo_sb = sbuf("xo_sb", [P, M], U32)
         nc.sync.dma_start(xo_sb[:].bitcast(I32), xo_words[0].rearrange("p n t -> p (n t)").bitcast(I32))
-        l5 = load_list("l5", offs5)
+        w2_sb = sbuf("w2_sb", [P, 2 * R], U8)
+        nc.sync.dma_start(w2_sb[:].bitcast(I32), w2_words[0].bitcast(I32))
         l6 = load_list("l6", offs6)
         sa_sb = load_column("sa_sb", sa)
         l7 = load_list("l7", offs7)
@@ -104,20 +107,22 @@ def tile_picked_basedetail_codes_bank_boardpair_one_plain_kernel(
             board.append(sbuf("board%d" % s, [P, C], F32))
             nc.vector.memset(board[s][:], 0.0)
 
-        wc_planes = sbuf("wc_planes", [P, PACK, R], BF16)
-        for t in range(PACK):
-            nc.scalar.activation(out=wc_planes[:, t, :], in_=ua_sb[t][:].indirect(l3[:]), func=ACT.Copy, scale=ha_sb[:, t : t + 1])
+        wc_in = sbuf("wc_in", [P, R * PACK], BF16)
+        for u in range(2):
+            wc_pair = sbuf("wc_pair%d" % u, [P, 2, R], BF16)
+            for e in range(2):
+                t = 2 * u + e
+                nc.scalar.activation(out=wc_pair[:, e, :], in_=ua_sb[t][:].indirect(l3[:]), func=ACT.Copy, scale=ha_sb[:, t : t + 1])
+            nc.vector.tensor_copy(
+                out=wc_in[:].rearrange("p (s m t) -> p m t s", s=PACK, t=PACK)[:, :, 2 * u : 2 * u + 2, :],
+                in_=wc_pair[:].rearrange("p t (m s) -> p m t s", s=PACK),
+            )
         w2_scd = sbuf("w2_scd", [P, R], U8)
         nc.vector.tensor_copy(
             out=w2_scd[:].rearrange("p (s m) -> p s m", s=PACK), in_=w2_sc[:].rearrange("p (m s) -> p s m", s=PACK)
         )
         xo_gsc = sbuf("xo_gsc", [P, J], U8)
         nc.vector.tensor_copy(out=xo_gsc[:], in_=xo_sc[:].indirect(l4[:]))
-        wc_in = sbuf("wc_in", [P, R * PACK], BF16)
-        nc.vector.tensor_copy(
-            out=wc_in[:].rearrange("p (s m t) -> p m t s", s=PACK, t=PACK),
-            in_=wc_planes[:].rearrange("p t (m s) -> p m t s", s=PACK),
-        )
         wc_q = sbuf("wc_q", [P, R], U32)
         wc_sc = sbuf("wc_sc", [P, R], U8)
         nc.vector.quantize_mx(out=wc_q[:].bitcast(FP8X4), scales=wc_sc[:], in_=wc_in[:])
@@ -136,30 +141,29 @@ def tile_picked_basedetail_codes_bank_boardpair_one_plain_kernel(
                 in1=det01[:, :, cols].rearrange("p t j -> p j t"),
                 op=ALU.add,
             )
-        base2 = sbuf("base2", [P, J], F32)
-        det2 = sbuf("det2", [P, J], F32)
-        base3 = sbuf("base3", [P, J], F32)
-        nc.scalar.activation(out=base2[:], in_=ta_sb[2][:].indirect(l1[:]), func=ACT.Copy, scale=ga_sb[:, 2:3])
-        nc.scalar.activation(out=det2[:], in_=tb_sb[2][:].indirect(l2[:]), func=ACT.Copy, scale=gb_sb[:, 2:3])
-        for h in range(2):
-            cols = slice(h * HALF, (h + 1) * HALF)
-            nc.vector.tensor_tensor(out=xc_in[h][:, :, 2], in0=base2[:, cols], in1=det2[:, cols], op=ALU.add)
-        nc.scalar.activation(out=base3[:], in_=ta_sb[3][:].indirect(l1[:]), func=ACT.Copy, scale=ga_sb[:, 3:4])
-        det3 = [sbuf("det3_%d" % h, [P, HALF], F32) for h in range(2)]
+        base23 = sbuf("base23", [P, 3, HALF], F32)
+        det23 = sbuf("det23", [P, 3, HALF], F32)
+        nc.scalar.activation(
+            out=base23[:, 0:2, :].rearrange("p h j -> p (h j)"), in_=ta_sb[2][:].indirect(l1[:]), func=ACT.Copy, scale=ga_sb[:, 2:3]
+        )
+        nc.scalar.activation(
+            out=det23[:, 0:2, :].rearrange("p h j -> p (h j)"), in_=tb_sb[2][:].indirect(l2[:]), func=ACT.Copy, scale=gb_sb[:, 2:3]
+        )
         for h in range(2):
             nc.scalar.activation(
-                out=det3[h][:], in_=tb_sb[3][:].indirect(l2[:, 8 * h : 8 * h + 8]), func=ACT.Copy, scale=gb_sb[:, 3:4]
+                out=base23[:, 2, :], in_=ta_sb[3][:].indirect(l1[:, 8 * h : 8 * h + 8]), func=ACT.Copy, scale=ga_sb[:, 3:4]
             )
-        for h in range(2):
-            cols = slice(h * HALF, (h + 1) * HALF)
-            nc.vector.tensor_tensor(out=xc_in[h][:, :, 3], in0=base3[:, cols], in1=det3[h][:], op=ALU.add)
+            nc.scalar.activation(
+                out=det23[:, 2, :], in_=tb_sb[3][:].indirect(l2[:, 8 * h : 8 * h + 8]), func=ACT.Copy, scale=gb_sb[:, 3:4]
+            )
+            nc.vector.tensor_tensor(
+                out=xc_in[h][:, :, 2:4],
+                in0=base23[:, h : 3 : 2 - h, :].rearrange("p t j -> p j t"),
+                in1=det23[:, h : 3 : 2 - h, :].rearrange("p t j -> p j t"),
+                op=ALU.add,
+            )
 
-        w2_d = sbuf("w2_d", [P, 2 * R], U8)
-        nc.scalar.copy(
-            out=w2_d[:].bitcast(U16).rearrange("p (s m) -> p s m", s=PACK),
-            in_=w2_sb[:].bitcast(U16).rearrange("p (m s) -> p s m", s=PACK),
-        )
-
+        w2_d = []
         xc_q = sbuf("xc_q", [P, J], U32)
         xc_sc = sbuf("xc_sc", [P, J], U8)
         xo_g = sbuf("xo_g", [P, J], U32)
@@ -176,17 +180,20 @@ def tile_picked_basedetail_codes_bank_boardpair_one_plain_kernel(
         second_last = sbuf("second_last", [P, O], F32)
         firsts = [first[:, s, :] for s in range(PACK - 1)] + [first_last[:]]
         seconds = [second[:, s, :] for s in range(PACK - 1)] + [second_last[:]]
-        pieces = [(0, 0, HALF), (0, HALF, J)] + [(s, 0, J) for s in range(1, PACK)]
+        pieces = [(s, h * HALF, (h + 1) * HALF) for h in range(2) for s in range(2)] + [(s, 0, J) for s in range(2, PACK)]
         hidden = []
         for i, (s, j0, j1) in enumerate(pieces):
             rows = slice(s * P, (s + 1) * P)
+            if j0 == 0:
+                w2_d.append(keep.tile([P, 2 * P], U8, name="w2_d%d" % s, tag="w2_d", bufs=2, align_bytes=64))
+                nc.scalar.copy(out=w2_d[s][:].bitcast(U16), in_=w2_sb[:].bitcast(U16).rearrange("p (m s) -> p s m", s=PACK)[:, s, :])
             acc = psum.tile([P, j1 - j0], F32, name="acc%d" % i, tag="acc", bufs=2)
             nc.tensor.matmul_mx(
                 out=acc[:], lhsT=wc_q[:, rows].bitcast(FP8X4), lhsT_scale=wc_sc[:, rows],
                 rhs=xc_q[:, j0:j1].bitcast(FP8X4), rhs_scale=xc_sc[:, j0:j1], start=True, stop=False,
             )
             nc.tensor.matmul_mx(
-                out=acc[:], lhsT=w2_d[:, 2 * s * P : 2 * (s + 1) * P].bitcast(FP4X4), lhsT_scale=w2_scd[:, rows],
+                out=acc[:], lhsT=w2_d[s][:].bitcast(FP4X4), lhsT_scale=w2_scd[:, rows],
                 rhs=xo_g[:, j0:j1].bitcast(FP8X4), rhs_scale=xo_gsc[:, j0:j1], start=False, stop=True,
             )
             hidden.append(keep.tile([P, j1 - j0], F32, name="hidden%d" % i, tag="hidden", bufs=2, align_bytes=64))

from contextlib import ExitStack

import concourse.mybir as mybir

K, J, R, T, U, F, Z, M, O, C, N = 512, 256, 512, 512, 512, 2048, 512, 1024, 128, 512, 256
FLOPS = 2 * (K * R * J + Z * R * J + R * N * O)

F32 = mybir.dt.float32
BF16 = mybir.dt.bfloat16
I32 = mybir.dt.int32
U32 = mybir.dt.uint32
U16 = mybir.dt.uint16
U8 = mybir.dt.uint8
FP8X4 = mybir.dt.float8_e4m3fn_x4
FP4X4 = mybir.dt.float4_e2m1fn_x4
ACT = mybir.ActivationFunctionType
ALU = mybir.AluOpType

P = 128
PACK = 4
HALF = J // 2


def tile_picked_basedetail_codes_bank_boardpair_one_plain_kernel(
    tc, ta, tb, ga, gb, ua, ha, xo_words, xo_scales, w2_words, w2_scales, sa, sb, wb_words, wb_scales,
    offs, offs2, offs3, offs4, offs5, offs6, offs7, out,
):
    nc = tc.nc
    with ExitStack() as ctx:
        keep = ctx.enter_context(tc.tile_pool(name="keep", bufs=1))
        psum = ctx.enter_context(tc.psum_pool(name="psum", bufs=1))

        def sbuf(name, shape, dtype):
            return keep.tile(shape, dtype, name=name, align_bytes=64)

        def load_list(name, src):
            tile = sbuf(name, list(src.shape), U16)
            nc.sync.dma_start(tile[:], src)
            return tile

        def load_column(name, src):
            tile = sbuf(name, [P, PACK], F32)
            nc.sync.dma_start(tile[:], src.rearrange("(p t) o -> p (t o)", t=PACK))
            return tile

        def load_rows(name, src, t):
            tile = sbuf(name, [P, src.shape[1]], F32)
            nc.sync.dma_start(tile[:], src.rearrange("(p t) c -> p t c", t=PACK)[:, t, :])
            return tile

        def load_scales(name, src, queue):
            tile = sbuf(name, [P, src.shape[2]], U8)
            nc.vector.memset(tile[:].bitcast(I32), 0)
            for q in range(4):
                queue.dma_start(tile[32 * q : 32 * q + 4, :].bitcast(I32), src[0, 4 * q : 4 * q + 4, :].bitcast(I32))
            return tile

        def stage_scales(name, src):
            width = src.shape[2]
            stage = sbuf(name + "_stage", [P, 2, width // 4], I32)
            for u in range(2):
                rows = src[0, 8 * u : 8 * u + 8, :].bitcast(I32).rearrange("(q r) c -> r q c", q=2)
                nc.gpsimd.dma_start(stage[64 * u : 64 * u + 4, :, :], rows)
            tile = sbuf(name, [P, width], U8)
            nc.vector.memset(tile[:].bitcast(I32), 0)
            for q in range(4):
                u = q // 2
                nc.vector.tensor_copy(out=tile[32 * q : 32 * q + 4, :].bitcast(I32), in_=stage[64 * u : 64 * u + 4, q % 2, :])
            return tile

        w2_sc = stage_scales("w2_sc", w2_scales)
        xo_sc = stage_scales("xo_sc", xo_scales)

        ua_sb = [load_rows("ua0", ua, 0)]
        l3 = load_list("l3", offs3)
        ha_sb = load_column("ha_sb", ha)
        ua_sb.append(load_rows("ua1", ua, 1))
        l1 = load_list("l1", offs)
        ga_sb = load_column("ga_sb", ga)
        ta_sb = [load_rows("ta0", ta, 0)]
        ua_sb.append(load_rows("ua2", ua, 2))
        l2 = load_list("l2", offs2)
        gb_sb = load_column("gb_sb", gb)
        tb_sb = [load_rows("tb0", tb, 0)]
        ta_sb.append(load_rows("ta1", ta, 1))
        tb_sb.append(load_rows("tb1", tb, 1))
        ua_sb.append(load_rows("ua3", ua, 3))
        l4 = load_list("l4", offs4)
        l5 = load_list("l5", offs5)
        for t in range(2, PACK):
            ta_sb.append(load_rows("ta%d" % t, ta, t))
            tb_sb.append(load_rows("tb%d" % t, tb, t))
        xo_sb = sbuf("xo_sb", [P, M], U32)
        nc.sync.dma_start(xo_sb[:].bitcast(I32), xo_words[0].rearrange("p n t -> p (n t)").bitcast(I32))
        w2_sb = sbuf("w2_sb", [P, 2 * R], U8)
        nc.sync.dma_start(w2_sb[:].bitcast(I32), w2_words[0].bitcast(I32))
        l6 = load_list("l6", offs6)
        sa_sb = load_column("sa_sb", sa)
        l7 = load_list("l7", offs7)
        sb_sb = load_column("sb_sb", sb)
        wb_sb = sbuf("wb_sb", [P, 2 * N], U8)
        nc.sync.dma_start(wb_sb[:].bitcast(I32), wb_words[0].bitcast(I32))
        wb_sc = load_scales("wb_sc", wb_scales, nc.sync)

        board = []
        for s in range(PACK):
            board.append(sbuf("board%d" % s, [P, C], F32))
            nc.vector.memset(board[s][:], 0.0)

        wc_in = sbuf("wc_in", [P, R * PACK], BF16)
        for u in range(2):
            wc_pair = sbuf("wc_pair%d" % u, [P, 2, R], BF16)
            for e in range(2):
                t = 2 * u + e
                nc.scalar.activation(out=wc_pair[:, e, :], in_=ua_sb[t][:].indirect(l3[:]), func=ACT.Copy, scale=ha_sb[:, t : t + 1])
            nc.vector.tensor_copy(
                out=wc_in[:].rearrange("p (s m t) -> p m t s", s=PACK, t=PACK)[:, :, 2 * u : 2 * u + 2, :],
                in_=wc_pair[:].rearrange("p t (m s) -> p m t s", s=PACK),
            )
        w2_scd = sbuf("w2_scd", [P, R], U8)
        nc.vector.tensor_copy(
            out=w2_scd[:].rearrange("p (s m) -> p s m", s=PACK), in_=w2_sc[:].rearrange("p (m s) -> p s m", s=PACK)
        )
        xo_gsc = sbuf("xo_gsc", [P, J], U8)
        nc.vector.tensor_copy(out=xo_gsc[:], in_=xo_sc[:].indirect(l4[:]))
        wc_q = sbuf("wc_q", [P, R], U32)
        wc_sc = sbuf("wc_sc", [P, R], U8)
        nc.vector.quantize_mx(out=wc_q[:].bitcast(FP8X4), scales=wc_sc[:], in_=wc_in[:])

        xc_in = [sbuf("xc_in%d" % h, [P, HALF, PACK], BF16) for h in range(2)]
        base01 = sbuf("base01", [P, 2, J], F32)
        det01 = sbuf("det01", [P, 2, J], F32)
        for t in range(2):
            nc.scalar.activation(out=base01[:, t, :], in_=ta_sb[t][:].indirect(l1[:]), func=ACT.Copy, scale=ga_sb[:, t : t + 1])
            nc.scalar.activation(out=det01[:, t, :], in_=tb_sb[t][:].indirect(l2[:]), func=ACT.Copy, scale=gb_sb[:, t : t + 1])
        for h in range(2):
            cols = slice(h * HALF, (h + 1) * HALF)
            nc.vector.tensor_tensor(
                out=xc_in[h][:, :, 0:2],
                in0=base01[:, :, cols].rearrange("p t j -> p j t"),
                in1=det01[:, :, cols].rearrange("p t j -> p j t"),
                op=ALU.add,
            )
        base23 = sbuf("base23", [P, 3, HALF], F32)
        det23 = sbuf("det23", [P, 3, HALF], F32)
        nc.scalar.activation(
            out=base23[:, 0:2, :].rearrange("p h j -> p (h j)"), in_=ta_sb[2][:].indirect(l1[:]), func=ACT.Copy, scale=ga_sb[:, 2:3]
        )
        nc.scalar.activation(
            out=det23[:, 0:2, :].rearrange("p h j -> p (h j)"), in_=tb_sb[2][:].indirect(l2[:]), func=ACT.Copy, scale=gb_sb[:, 2:3]
        )
        for h in range(2):
            nc.scalar.activation(
                out=base23[:, 2, :], in_=ta_sb[3][:].indirect(l1[:, 8 * h : 8 * h + 8]), func=ACT.Copy, scale=ga_sb[:, 3:4]
            )
            nc.scalar.activation(
                out=det23[:, 2, :], in_=tb_sb[3][:].indirect(l2[:, 8 * h : 8 * h + 8]), func=ACT.Copy, scale=gb_sb[:, 3:4]
            )
            nc.vector.tensor_tensor(
                out=xc_in[h][:, :, 2:4],
                in0=base23[:, h : 3 : 2 - h, :].rearrange("p t j -> p j t"),
                in1=det23[:, h : 3 : 2 - h, :].rearrange("p t j -> p j t"),
                op=ALU.add,
            )

        w2_d = []
        xc_q = sbuf("xc_q", [P, J], U32)
        xc_sc = sbuf("xc_sc", [P, J], U8)
        xo_g = sbuf("xo_g", [P, J], U32)
        for h in range(2):
            cols = slice(h * HALF, (h + 1) * HALF)
            nc.vector.quantize_mx(
                out=xc_q[:, cols].bitcast(FP8X4), scales=xc_sc[:, cols], in_=xc_in[h][:].rearrange("p j t -> p (j t)")
            )
            nc.vector.tensor_copy(out=xo_g[:, cols], in_=xo_sb[:].indirect(l4[:, 8 * h : 8 * h + 8]))

        first = sbuf("first", [P, PACK - 1, O], F32)
        second = sbuf("second", [P, PACK - 1, O], F32)
        first_last = sbuf("first_last", [P, O], F32)
        second_last = sbuf("second_last", [P, O], F32)
        firsts = [first[:, s, :] for s in range(PACK - 1)] + [first_last[:]]
        seconds = [second[:, s, :] for s in range(PACK - 1)] + [second_last[:]]
        pieces = [(s, h * HALF, (h + 1) * HALF) for h in range(2) for s in range(2)] + [(s, 0, J) for s in range(2, PACK)]
        hidden = []
        for i, (s, j0, j1) in enumerate(pieces):
            rows = slice(s * P, (s + 1) * P)
            if j0 == 0:
                w2_d.append(keep.tile([P, 2 * P], U8, name="w2_d%d" % s, tag="w2_d", bufs=2, align_bytes=64))
                nc.scalar.copy(out=w2_d[s][:].bitcast(U16), in_=w2_sb[:].bitcast(U16).rearrange("p (m s) -> p s m", s=PACK)[:, s, :])
            acc = psum.tile([P, j1 - j0], F32, name="acc%d" % i, tag="acc", bufs=2)
            nc.tensor.matmul_mx(
                out=acc[:], lhsT=wc_q[:, rows].bitcast(FP8X4), lhsT_scale=wc_sc[:, rows],
                rhs=xc_q[:, j0:j1].bitcast(FP8X4), rhs_scale=xc_sc[:, j0:j1], start=True, stop=False,
            )
            nc.tensor.matmul_mx(
                out=acc[:], lhsT=w2_d[s][:].bitcast(FP4X4), lhsT_scale=w2_scd[:, rows],
                rhs=xo_g[:, j0:j1].bitcast(FP8X4), rhs_scale=xo_gsc[:, j0:j1], start=False, stop=True,
            )
            hidden.append(keep.tile([P, j1 - j0], F32, name="hidden%d" % i, tag="hidden", bufs=2, align_bytes=64))
            nc.scalar.copy(out=hidden[i][:], in_=acc[:])
            nc.vector.tensor_copy(out=board[s][:].indirect(l5[:, j0 // 16 : j1 // 16]), in_=hidden[i][:])
        for s in range(PACK):
            nc.scalar.activation(out=firsts[s], in_=board[s][:].indirect(l6[:]), func=ACT.Copy, scale=sa_sb[:, s : s + 1])
            nc.scalar.activation(out=seconds[s], in_=board[s][:].indirect(l7[:]), func=ACT.Copy, scale=sb_sb[:, s : s + 1])

        diff = sbuf("diff", [P, PACK, O], F32)
        nc.vector.tensor_tensor(out=diff[:, 0:3, :], in0=first[:], in1=second[:], op=ALU.subtract)
        nc.vector.tensor_tensor(out=diff[:, 3, :], in0=first_last[:], in1=second_last[:], op=ALU.subtract)
        hid_in = sbuf("hid_in", [P, O, PACK], BF16)
        for u in range(2):
            nc.scalar.activation(
                out=hid_in[:, :, 2 * u : 2 * u + 2], in_=diff[:, 2 * u : 2 * u + 2, :].rearrange("p s o -> p o s"), func=ACT.Abs
            )
        hid_q = sbuf("hid_q", [P, O], U32)
        hid_sc = sbuf("hid_sc", [P, O], U8)
        nc.vector.quantize_mx(out=hid_q[:].bitcast(FP8X4), scales=hid_sc[:], in_=hid_in[:].rearrange("p o s -> p (o s)"))

        for h in range(2):
            res = psum.tile([P, O], F32, name="res%d" % h)
            nc.tensor.matmul_mx(
                out=res[:], lhsT=wb_sb[:, 2 * h * P : 2 * (h + 1) * P].bitcast(FP4X4), lhsT_scale=wb_sc[:, h * P : (h + 1) * P],
                rhs=hid_q[:].bitcast(FP8X4), rhs_scale=hid_sc[:], start=True, stop=True,
            )
            res_sb = sbuf("res_sb%d" % h, [P, O], F32)
            if h == 0:
                nc.vector.tensor_copy(out=res_sb[:], in_=res[:])
                nc.sync.dma_start(out[h * P : (h + 1) * P, :], res_sb[:])
            else:
                nc.scalar.copy(out=res_sb[:], in_=res[:])
                nc.scalar.dma_start(out[h * P : (h + 1) * P, :], res_sb[:])
